import numpy as np
import ml_dtypes


def mxq(x, axis, fmt="e4m3"):
    dtype, down = {"e4m3": (ml_dtypes.float8_e4m3fn, 7), "e5m2": (ml_dtypes.float8_e5m2, 14)}[fmt]
    v = np.moveaxis(np.asarray(x, np.float32).astype(ml_dtypes.bfloat16).astype(np.float64), axis, -1)
    blocks = v.reshape(v.shape[:-1] + (-1, 32))
    amax = np.abs(blocks).max(-1, keepdims=True)
    byte = np.maximum(np.where(amax > 0, np.frexp(amax)[1] - 1 + 127, 0) - down, 1)
    scale = np.exp2(byte - 127.0)
    codes = (blocks / scale).astype(np.float32).astype(dtype).astype(np.float64)
    return np.moveaxis((codes * scale).reshape(v.shape), -1, axis)


WIDE = False


def mx_kscale(k):
    if not WIDE:
        return np.ones(k)
    levels = np.array([10, -10, 5, -5, 0])
    if k % 512:
        return np.exp2(np.random.permutation(np.resize(levels, k // 32))).repeat(32)
    a = np.empty((k // 512, 16))
    for p in range(k // 512):
        a[p, :8] = np.random.permutation(np.resize(levels, 8))
        for g in range(8):
            far = levels[np.abs(levels - a[p, g]) >= 10]
            a[p, g + 8] = far[np.random.randint(len(far))]
    return np.exp2(a.ravel()).repeat(32)


def f64(x):
    return np.asarray(x).astype(np.float64)


def striped(idx):
    return np.tile(np.asarray(idx).reshape(-1, 16).T, (8, 1)).astype(np.uint16)


def unstriped(offs):
    return offs[:16].T.reshape(-1).astype(np.int64)


def striped8(idx):
    return np.asarray(idx).reshape(8, -1, 16).transpose(0, 2, 1).reshape(128, -1).astype(np.uint16)


def unstriped8(offs):
    return offs.reshape(8, 16, -1).transpose(0, 2, 1).reshape(8, -1).astype(np.int64)


def pick8(x, idx, run):
    r = np.arange(len(x))
    return x[r[:, None], idx[r % (8 * run) // run]]


E2M1 = np.array([0.0, 0.5, 1.0, 1.5, 2.0, 3.0, 4.0, 6.0, -0.0, -0.5, -1.0, -1.5, -2.0, -3.0, -4.0, -6.0])


def pack_weight(w, fmt):
    k, n = w.shape
    w = f64(np.asarray(w, np.float32).astype(ml_dtypes.bfloat16)).reshape(k // 32, 32, n)
    amax = np.abs(w).max(1)
    if fmt == "e4m3":
        byte = np.frexp(amax)[1] - 1 + 127 - 7
    else:
        mant, ex = np.frexp(amax / 6.0)
        byte = np.where(mant > 0.5, ex, ex - 1) + 127
    byte = np.clip(np.where(amax > 0, byte, 1), 1, 254)
    scaled = (w * np.exp2(127.0 - byte)[:, None, :]).reshape(k, n).astype(np.float32)
    by_word = np.ascontiguousarray(scaled.reshape(k // 512, 128, 4, n).transpose(0, 1, 3, 2))
    if fmt == "e4m3":
        words = by_word.astype(ml_dtypes.float8_e4m3fn).view(np.uint8)
    else:
        c = by_word.astype(ml_dtypes.float4_e2m1fn).view(np.uint8) & 0xF
        words = (c[..., 0::2] | (c[..., 1::2] << 4)).reshape(k // 512, 128, 2 * n)
    return np.ascontiguousarray(words), np.ascontiguousarray(byte.astype(np.uint8).reshape(k // 512, 16, n))


def unpack_weight(words, scales, fmt):
    g, _, n = scales.shape
    words = np.ascontiguousarray(words).reshape(g, 128, n, -1)
    if fmt == "e4m3":
        vals = words.view(ml_dtypes.float8_e4m3fn).astype(np.float64)
    else:
        nib = np.empty((g, 128, n, 4), np.uint8)
        nib[..., 0::2] = words & 0xF
        nib[..., 1::2] = words >> 4
        vals = E2M1[nib]
    vals = vals * np.repeat(np.exp2(scales.astype(np.float64) - 127.0), 8, axis=1)[..., None]
    return vals.transpose(0, 1, 3, 2).reshape(g * 512, n)


K, J, R, T, Z, M, C, O, S, U, N, V = 512, 256, 512, 1024, 512, 1024, 512, 256, 128, 256, 256, 1024


def setup_inputs():
    n = np.random.standard_normal
    idx = np.random.permutation(T)[:J]
    idx2 = np.random.permutation(M)[:J]
    idx3 = np.stack([np.random.permutation(C)[:J] for _ in range(8)])
    idx4 = np.stack([np.random.permutation(J)[:S] for _ in range(8)])
    idx5 = np.stack([np.random.permutation(U)[:S] for _ in range(8)])
    idx6 = np.stack([np.random.permutation(C)[:O] for _ in range(8)])
    idx7 = np.random.permutation(V)[:N]
    fk = mx_kscale(K)
    fr = mx_kscale(R)
    fz = mx_kscale(Z)
    xtp = pack_weight(n((K, T)) * fk[:, None], "e4m3")
    wp = pack_weight(n((K, R)) * 1 / np.sqrt(K) / fk[:, None] * fr, "e2m1")
    xop = pack_weight(n((Z, M)) / fz[:, None], "e2m1")
    w2p = pack_weight(n((Z, R)) * 1 / np.sqrt(Z) * fz[:, None] * fr, "e4m3")
    vsp = pack_weight(n((R, V)) * 1 / np.sqrt(R) / fr[:, None], "e4m3")
    return {
        "xt_words": xtp[0],
        "xt_scales": xtp[1],
        "w_words": wp[0],
        "w_scales": wp[1],
        "xo_words": xop[0],
        "xo_scales": xop[1],
        "w2_words": w2p[0],
        "w2_scales": w2p[1],
        "sa": (np.random.uniform(0.5, 1.6, (R, 1))).astype(np.float32),
        "sb": (np.random.uniform(0.5, 1.6, (R, 1))).astype(np.float32),
        "vs_words": vsp[0],
        "vs_scales": vsp[1],
        "offs": striped(idx),
        "offs2": striped(idx2),
        "offs3": striped8(idx3),
        "offs4": striped8(idx4),
        "offs5": striped8(idx5),
        "offs6": striped8(idx6),
        "offs7": striped(idx7),
    }


def reference(xt_words, xt_scales, w_words, w_scales, xo_words, xo_scales, w2_words, w2_scales, sa, sb, vs_words, vs_scales, offs, offs2, offs3, offs4, offs5, offs6, offs7):
    idx = unstriped(offs)
    idx2 = unstriped(offs2)
    idx3 = unstriped8(offs3)
    idx4 = unstriped8(offs4)
    idx5 = unstriped8(offs5)
    idx6 = unstriped8(offs6)
    idx7 = unstriped(offs7)
    xtu = unpack_weight(xt_words, xt_scales, "e4m3")
    wu = unpack_weight(w_words, w_scales, "e2m1")
    xou = unpack_weight(xo_words, xo_scales, "e2m1")
    w2u = unpack_weight(w2_words, w2_scales, "e4m3")
    vsu = unpack_weight(vs_words, vs_scales, "e4m3")
    xtidxg = xtu[:, idx]
    xoidx2g = xou[:, idx2]
    a = wu.T @ xtidxg + w2u.T @ xoidx2g
    pw = np.zeros((R, C))
    pw[np.arange(R)[:, None], idx3[np.arange(R) % 512 // 64]] = a
    h1 = pick8(a, idx4, 64) * f64(sa)
    pu = np.zeros((R, U))
    pu[np.arange(R)[:, None], idx5[np.arange(R) % 512 // 64]] = h1
    g1 = np.repeat(pu, C // U, axis=1)
    pg = np.maximum(pw, g1)
    hid = pick8(pg, idx6, 64) * f64(sb)
    vsidx7g = vsu[:, idx7]
    hidq = mxq(hid, 0, "e4m3")
    y = vsidx7g.T @ hidq
    return y

@@ -1,0 +1,236 @@
+from contextlib import ExitStack
+
+import concourse.mybir as mybir
+
+K, J, R, T, Z, M, C, O, S, U, N, V = 512, 256, 512, 1024, 512, 1024, 512, 256, 128, 256, 256, 1024
+FLOPS = 2 * (K * R * J + Z * R * J + R * N * O)
+
+F32 = mybir.dt.float32
+BF16 = mybir.dt.bfloat16
+I32 = mybir.dt.int32
+U32 = mybir.dt.uint32
+U16 = mybir.dt.uint16
+U8 = mybir.dt.uint8
+FP8X4 = mybir.dt.float8_e4m3fn_x4
+FP4X4 = mybir.dt.float4_e2m1fn_x4
+COPY = mybir.ActivationFunctionType.Copy
+MAX = mybir.AluOpType.max
+
+P = 128
+PACK = 4
+HALF = 128
+LIST_ROWS = 16
+
+
+def tile_picked_tokens_plain_bank_coarsefine_store_plain_kernel(
+    tc, xt_words, xt_scales, w_words, w_scales, xo_words, xo_scales, w2_words, w2_scales, sa, sb,
+    vs_words, vs_scales, offs, offs2, offs3, offs4, offs5, offs6, offs7, out,
+):
+    nc = tc.nc
+    with ExitStack() as ctx:
+        keep = ctx.enter_context(tc.tile_pool(name="keep", bufs=1))
+        psum = ctx.enter_context(tc.psum_pool(name="psum", bufs=1))
+
+        def sbuf(name, shape, dtype):
+            return keep.tile(shape, dtype, name=name, align_bytes=64)
+
+        def load_list(name, src):
+            lst = keep.tile(list(src.shape), U16, name=name)
+            nc.sync.dma_start(lst[:], src)
+            return lst
+
+        def entries(lst, first, count):
+            return lst[:, first // LIST_ROWS:(first + count) // LIST_ROWS]
+
+        def load_words(queue, name, src, cols, dtype):
+            words = sbuf(name, [P, cols], dtype)
+            queue.dma_start(out=words[:].bitcast(I32), in_=src.bitcast(I32))
+            return words
+
+        def load_scale_rows(queue, stage, base, src, b):
+            rows = src[0].bitcast(I32).rearrange("(a b j) n -> b j a n", a=2, b=2)
+            queue.dma_start(out=stage[base + 32 * b:base + 32 * b + 4, :, :], in_=rows[b])
+
+        def e4m3_rows(src):
+            return src[0].rearrange("p n t -> p (n t)")
+
+        xt_stage = sbuf("xt_stage", [64, 2, T // 4], I32)
+        xo_stage = sbuf("xo_stage", [64, 2, M // 4], I32)
+        w_plane = sbuf("w_plane", [P, 2, R // 4], I32)
+        w2_plane = sbuf("w2_plane", [P, 2, R // 4], I32)
+        vs_stage = sbuf("vs_stage", [64, 2, V // 4], I32)
+        nc.vector.memset(xt_stage[:], 0)
+        nc.gpsimd.memset(xo_stage[:], 0)
+        nc.vector.memset(w_plane[64:P], 0)
+        nc.vector.memset(w2_plane[64:P], 0)
+
+        tok_list = load_list("tok_list", offs)
+        w_raw = load_words(nc.scalar, "w_raw", w_words[0], R, U16)
+        note_list = load_list("note_list", offs2)
+        w2_raw = load_words(nc.scalar, "w2_raw", e4m3_rows(w2_words), R, U32)
+        for b in range(2):
+            load_scale_rows(nc.sync, xt_stage, 0, xt_scales, b)
+            load_scale_rows(nc.scalar, xo_stage, 0, xo_scales, b)
+        xt_table = load_words(nc.scalar, "xt_table", e4m3_rows(xt_words), T, U32)
+        for plane, src in ((w_plane, w_scales), (w2_plane, w2_scales)):
+            for b in range(2):
+                load_scale_rows(nc.sync, plane, 64, src, b)
+        xo_table = load_words(nc.sync, "xo_table", xo_words[0], M, U16)
+        fine_list = load_list("fine_list", offs3)
+        pick_list = load_list("pick_list", offs4)
+        sa_cols = sbuf("sa_cols", [P, PACK], F32)
+        nc.sync.dma_start(out=sa_cols[:], in_=sa.rearrange("(p t) o -> p (t o)", t=PACK))
+        coarse_list = load_list("coarse_list", offs5)
+        store_list = load_list("store_list", offs7)
+        nc.vector.memset(vs_stage[:], 0)
+        vs_table = load_words(nc.sync, "vs_table", e4m3_rows(vs_words), V, U32)
+        for b in range(2):
+            load_scale_rows(nc.sync, vs_stage, 0, vs_scales, b)
+        sb_cols = sbuf("sb_cols", [P, PACK], F32)
+        nc.sync.dma_start(out=sb_cols[:], in_=sb.rearrange("(p t) o -> p (t o)", t=PACK))
+        read_list = load_list("read_list", offs6)
+
+        fine = [sbuf(f"fine{i}", [P, C], F32) for i in range(2)]
+        coarse = [sbuf(f"coarse{i}", [P, U], F32) for i in range(2)]
+        for i in range(2):
+            nc.vector.memset(fine[i][:], 0.0)
+            nc.vector.memset(coarse[i][:], 0.0)
+
+        w_dealt = sbuf("w_dealt", [P, R], U16)
+        w2_dealt = sbuf("w2_dealt", [P, R], U32)
+
+        def deal_words(dealt, raw, t0, t1):
+            nc.scalar.copy(
+                out=dealt[:, t0 * P:t1 * P].rearrange("p (t m) -> p t m", m=P),
+                in_=raw[:].rearrange("p (m t) -> p t m", t=PACK)[:, t0:t1, :],
+            )
+
+        deal_words(w_dealt, w_raw, 0, PACK)
+        deal_words(w2_dealt, w2_raw, 0, PACK)
+
+        def spread(table, stage, a):
+            nc.vector.tensor_copy(out=table[64 * a:64 * a + 64, :].bitcast(I32), in_=stage[:, a, :])
+
+        def gather(dst, table, lst, first, count):
+            nc.vector.tensor_copy(dst[:, first:first + count], table[:].indirect(entries(lst, first, count)))
+
+        xt_codes = sbuf("xt_codes", [P, J], U32)
+        xt_bytes = sbuf("xt_bytes", [P, J], U8)
+        xo_codes = sbuf("xo_codes", [P, J], U16)
+        xo_bytes = sbuf("xo_bytes", [P, J], U8)
+
+        xt_scale_table = sbuf("xt_scale_table", [P, T], U8)
+        xo_scale_table = sbuf("xo_scale_table", [P, M], U8)
+        for a in range(2):
+            spread(xt_scale_table, xt_stage, a)
+            spread(xo_scale_table, xo_stage, a)
+        gather(xt_bytes, xt_scale_table, tok_list, 0, J)
+        gather(xo_bytes, xo_scale_table, note_list, 0, J)
+        gather(xt_codes, xt_table, tok_list, 0, HALF)
+        for plane in (w_plane, w2_plane):
+            nc.vector.tensor_copy(out=plane[0:64, 1, :], in_=plane[64:P, 0, :])
+
+        w_bytes = sbuf("w_bytes", [P, R], U8)
+        w2_bytes = sbuf("w2_bytes", [P, R], U8)
+
+        def deal_bytes(t0, t1):
+            for dealt, plane in ((w_bytes, w_plane), (w2_bytes, w2_plane)):
+                nc.vector.tensor_copy(
+                    out=dealt[:, t0 * P:t1 * P].rearrange("p (t m) -> p t m", m=P),
+                    in_=plane[:, 1, :].bitcast(U8).rearrange("p (m t) -> p t m", t=PACK)[:, t0:t1, :],
+                )
+
+        hidden = [sbuf(f"hidden{t}", [P, J], F32) for t in range(PACK)]
+
+        def first_product(t, first, count, copy):
+            acc = psum.tile([P, count], F32, name=f"acc{t}_{first}")
+            rows = slice(t * P, (t + 1) * P)
+            cols = slice(first, first + count)
+            nc.tensor.matmul_mx(
+                acc[:], lhsT=w_dealt[:, rows].bitcast(FP4X4), lhsT_scale=w_bytes[:, rows],
+                rhs=xt_codes[:, cols].bitcast(FP8X4), rhs_scale=xt_bytes[:, cols], start=True, stop=False,
+            )
+            nc.tensor.matmul_mx(
+                acc[:], lhsT=w2_dealt[:, rows].bitcast(FP8X4), lhsT_scale=w2_bytes[:, rows],
+                rhs=xo_codes[:, cols].bitcast(FP4X4), rhs_scale=xo_bytes[:, cols], start=False, stop=True,
+            )
+            copy(out=hidden[t][:, cols], in_=acc[:])
+
+        def put_fine(t, first, count):
+            nc.scalar.activation(
+                fine[t % 2][:].indirect(entries(fine_list, first, count)), hidden[t][:, first:first + count], COPY
+            )
+
+        deal_bytes(0, 1)
+        gather(xo_codes, xo_table, note_list, 0, HALF)
+        first_product(0, 0, HALF, nc.scalar.copy)
+        put_fine(0, 0, HALF)
+        gather(xt_codes, xt_table, tok_list, HALF, HALF)
+        gather(xo_codes, xo_table, note_list, HALF, HALF)
+        first_product(0, HALF, HALF, nc.vector.tensor_copy)
+        deal_bytes(1, PACK)
+        for t in range(1, PACK):
+            first_product(t, 0, J, nc.vector.tensor_copy)
+
+        vs_codes = sbuf("vs_codes", [P, N], U32)
+        vs_bytes = sbuf("vs_bytes", [P, N], U8)
+        vs_scale_table = sbuf("vs_scale_table", [P, V], U8)
+        for a in range(2):
+            spread(vs_scale_table, vs_stage, a)
+        gather(vs_bytes, vs_scale_table, store_list, 0, N)
+        gather(vs_codes, vs_table, store_list, 0, N)
+
+        larger = [sbuf(f"larger{t}", [P, C], F32) for t in range(PACK)]
+        picked = [sbuf(f"picked{t}", [P, S], F32) for t in range(PACK)]
+        for t in range(PACK):
+            nc.scalar.activation(picked[t][:], hidden[t][:].indirect(pick_list[:]), COPY, scale=sa_cols[:, t:t + 1])
+            if t == 0:
+                put_fine(t, HALF, HALF)
+            else:
+                put_fine(t, 0, J)
+            nc.scalar.activation(coarse[t % 2][:].indirect(coarse_list[:]), picked[t][:], COPY)
+            nc.vector.tensor_tensor(
+                out=larger[t][:].rearrange("p (u e) -> p u e", e=C // U),
+                in0=fine[t % 2][:].rearrange("p (u e) -> p u e", e=C // U),
+                in1=coarse[t % 2][:].unsqueeze(2).to_broadcast([P, U, C // U]),
+                op=MAX,
+            )
+
+        out_rows = out.rearrange("(b p) o -> p b o", p=P)
+        for h in range(2):
+            cols = slice(h * HALF, (h + 1) * HALF)
+            planes = sbuf(f"planes{h}", [P, PACK, HALF], BF16)
+            for t in range(PACK):
+                nc.scalar.activation(
+                    planes[:, t, :], larger[t][:].indirect(entries(read_list, h * HALF, HALF)), COPY,
+                    scale=sb_cols[:, t:t + 1],
+                )
+            woven = sbuf(f"woven{h}", [P, HALF, PACK], BF16)
+            nc.vector.tensor_copy(out=woven[:], in_=planes[:].rearrange("p t o -> p o t"))
+            hid_codes = sbuf(f"hid_codes{h}", [P, HALF], U32)
+            hid_bytes = sbuf(f"hid_bytes{h}", [P, HALF], U8)
+            nc.vector.quantize_mx(
+                out=hid_codes[:].bitcast(FP8X4), scales=hid_bytes[:], in_=woven[:].rearrange("p o t -> p (o t)")
+            )
+
+            def second_product(acc, b):
+                rows = slice(b * P, (b + 1) * P)
+                nc.tensor.matmul_mx(
+                    acc, lhsT=vs_codes[:, rows].bitcast(FP8X4), lhsT_scale=vs_bytes[:, rows],
+                    rhs=hid_codes[:].bitcast(FP8X4), rhs_scale=hid_bytes[:], start=True, stop=True,
+                )
+
+            if h == 0:
+                acc = psum.tile([P, 2, HALF], F32, name="y_first")
+                for b in range(2):
+                    second_product(acc[:, b, :], b)
+                result = sbuf("result_first", [P, 2, HALF], F32)
+                nc.scalar.copy(out=result[:], in_=acc[:])
+                nc.sync.dma_start(out=out_rows[:, :, cols], in_=result[:])
+            else:
+                for b, copy, queue in ((0, nc.vector.tensor_copy, nc.sync), (1, nc.scalar.copy, nc.scalar)):
+                    acc = psum.tile([P, HALF], F32, name=f"y_last{b}")
+                    second_product(acc[:], b)
+                    result = sbuf(f"result_last{b}", [P, HALF], F32)
+                    copy(out=result[:], in_=acc[:])
+                    queue.dma_start(out=out_rows[:, b, cols], in_=result[:])

@@ -29,6 +29,7 @@ def tile_picked_tokens_plain_bank_coarsefine_store_plain_kernel(
     nc = tc.nc
     with ExitStack() as ctx:
         keep = ctx.enter_context(tc.tile_pool(name="keep", bufs=1))
+        reused = ctx.enter_context(tc.tile_pool(name="reused", bufs=1))
         psum = ctx.enter_context(tc.psum_pool(name="psum", bufs=1))
 
         def sbuf(name, shape, dtype):
@@ -54,40 +55,47 @@ def tile_picked_tokens_plain_bank_coarsefine_store_plain_kernel(
         def e4m3_rows(src):
             return src[0].rearrange("p n t -> p (n t)")
 
+        def on_reused_bytes(name, shape, dtype, offset):
+            return reused.tile(shape, dtype, name=name, align_bytes=64, offset=offset)
+
         xt_stage = sbuf("xt_stage", [64, 2, T // 4], I32)
-        xo_stage = sbuf("xo_stage", [64, 2, M // 4], I32)
+        xo_stage = sbuf("xo_stage", [P, 2, M // 4], I32)
         w_plane = sbuf("w_plane", [P, 2, R // 4], I32)
-        w2_plane = sbuf("w2_plane", [P, 2, R // 4], I32)
+        w2_stage = on_reused_bytes("w2_stage", [64, 2, R // 4], I32, 320)
         vs_stage = sbuf("vs_stage", [64, 2, V // 4], I32)
         nc.vector.memset(xt_stage[:], 0)
-        nc.gpsimd.memset(xo_stage[:], 0)
+        nc.gpsimd.memset(xo_stage[64:P], 0)
         nc.vector.memset(w_plane[64:P], 0)
-        nc.vector.memset(w2_plane[64:P], 0)
+        nc.vector.memset(w2_stage[:], 0)
+        nc.vector.memset(vs_stage[:], 0)
+
+        def load_columns(name, src):
+            cols = sbuf(name, [P, PACK], F32)
+            nc.sync.dma_start(out=cols[:], in_=src.rearrange("(p t) o -> p (t o)", t=PACK))
+            return cols
 
         tok_list = load_list("tok_list", offs)
-        w_raw = load_words(nc.scalar, "w_raw", w_words[0], R, U16)
-        note_list = load_list("note_list", offs2)
-        w2_raw = load_words(nc.scalar, "w2_raw", e4m3_rows(w2_words), R, U32)
+        w_raw = load_words(nc.sync, "w_raw", w_words[0], R, U16)
         for b in range(2):
+            load_scale_rows(nc.scalar, xo_stage, 64, xo_scales, b)
             load_scale_rows(nc.sync, xt_stage, 0, xt_scales, b)
-            load_scale_rows(nc.scalar, xo_stage, 0, xo_scales, b)
-        xt_table = load_words(nc.scalar, "xt_table", e4m3_rows(xt_words), T, U32)
-        for plane, src in ((w_plane, w_scales), (w2_plane, w2_scales)):
-            for b in range(2):
-                load_scale_rows(nc.sync, plane, 64, src, b)
+        xt_table = load_words(nc.sync, "xt_table", e4m3_rows(xt_words), T, U32)
         xo_table = load_words(nc.sync, "xo_table", xo_words[0], M, U16)
+        note_list = load_list("note_list", offs2)
+        for b in range(2):
+            load_scale_rows(nc.sync, w_plane, 64, w_scales, b)
+        for b in range(2):
+            load_scale_rows(nc.sync, w2_stage, 0, w2_scales, b)
+        w2_raw = load_words(nc.sync, "w2_raw", e4m3_rows(w2_words), R, U32)
         fine_list = load_list("fine_list", offs3)
         pick_list = load_list("pick_list", offs4)
-        sa_cols = sbuf("sa_cols", [P, PACK], F32)
-        nc.sync.dma_start(out=sa_cols[:], in_=sa.rearrange("(p t) o -> p (t o)", t=PACK))
-        coarse_list = load_list("coarse_list", offs5)
-        store_list = load_list("store_list", offs7)
-        nc.vector.memset(vs_stage[:], 0)
-        vs_table = load_words(nc.sync, "vs_table", e4m3_rows(vs_words), V, U32)
+        sa_cols = load_columns("sa_cols", sa)
         for b in range(2):
             load_scale_rows(nc.sync, vs_stage, 0, vs_scales, b)
-        sb_cols = sbuf("sb_cols", [P, PACK], F32)
-        nc.sync.dma_start(out=sb_cols[:], in_=sb.rearrange("(p t) o -> p (t o)", t=PACK))
+        store_list = load_list("store_list", offs7)
+        vs_table = load_words(nc.sync, "vs_table", e4m3_rows(vs_words), V, U32)
+        coarse_list = load_list("coarse_list", offs5)
+        sb_cols = load_columns("sb_cols", sb)
         read_list = load_list("read_list", offs6)
 
         fine = [sbuf(f"fine{i}", [P, C], F32) for i in range(2)]
@@ -101,84 +109,95 @@ def tile_picked_tokens_plain_bank_coarsefine_store_plain_kernel(
 
         def deal_words(dealt, raw, t0, t1):
             nc.scalar.copy(
-                out=dealt[:, t0 * P:t1 * P].rearrange("p (t m) -> p t m", m=P),
-                in_=raw[:].rearrange("p (m t) -> p t m", t=PACK)[:, t0:t1, :],
+                out=dealt[:].rearrange("p (t m) -> p m t", t=PACK)[:, :, t0:t1],
+                in_=raw[:].rearrange("p (m t) -> p m t", t=PACK)[:, :, t0:t1],
             )
 
         deal_words(w_dealt, w_raw, 0, PACK)
-        deal_words(w2_dealt, w2_raw, 0, PACK)
+        deal_words(w2_dealt, w2_raw, 0, 1)
+        deal_words(w2_dealt, w2_raw, 1, PACK)
 
-        def spread(table, stage, a):
-            nc.vector.tensor_copy(out=table[64 * a:64 * a + 64, :].bitcast(I32), in_=stage[:, a, :])
+        def spread(plane, stage, base, halves):
+            for a in halves:
+                nc.vector.tensor_copy(out=plane[64 * a:64 * a + 64, :].bitcast(I32), in_=stage[base:base + 64, a, :])
 
         def gather(dst, table, lst, first, count):
-            nc.vector.tensor_copy(dst[:, first:first + count], table[:].indirect(entries(lst, first, count)))
+            nc.vector.tensor_copy(dst, table[:].indirect(entries(lst, first, count)))
 
-        xt_codes = sbuf("xt_codes", [P, J], U32)
+        def deal_bytes(dealt, plane, t0, t1):
+            nc.vector.tensor_copy(
+                out=dealt[:].rearrange("p (t m) -> p t m", m=P),
+                in_=plane.rearrange("p (m t) -> p t m", t=PACK)[:, t0:t1, :],
+            )
+
+        xt_codes = [sbuf("xt_codes0", [P, HALF], U32), on_reused_bytes("xt_codes1", [P, HALF], U32, 384)]
+        xo_codes = [sbuf("xo_codes0", [P, HALF], U16), on_reused_bytes("xo_codes1", [P, HALF], U16, 896)]
         xt_bytes = sbuf("xt_bytes", [P, J], U8)
-        xo_codes = sbuf("xo_codes", [P, J], U16)
         xo_bytes = sbuf("xo_bytes", [P, J], U8)
+        w_bytes = [sbuf("w_bytes0", [P, P], U8), on_reused_bytes("w_bytes1", [P, R - P], U8, 1152)]
+        w2_bytes = [sbuf("w2_bytes0", [P, P], U8), on_reused_bytes("w2_bytes1", [P, R - P], U8, 0)]
 
         xt_scale_table = sbuf("xt_scale_table", [P, T], U8)
         xo_scale_table = sbuf("xo_scale_table", [P, M], U8)
-        for a in range(2):
-            spread(xt_scale_table, xt_stage, a)
-            spread(xo_scale_table, xo_stage, a)
-        gather(xt_bytes, xt_scale_table, tok_list, 0, J)
-        gather(xo_bytes, xo_scale_table, note_list, 0, J)
-        gather(xt_codes, xt_table, tok_list, 0, HALF)
-        for plane in (w_plane, w2_plane):
-            nc.vector.tensor_copy(out=plane[0:64, 1, :], in_=plane[64:P, 0, :])
-
-        w_bytes = sbuf("w_bytes", [P, R], U8)
-        w2_bytes = sbuf("w2_bytes", [P, R], U8)
-
-        def deal_bytes(t0, t1):
-            for dealt, plane in ((w_bytes, w_plane), (w2_bytes, w2_plane)):
-                nc.vector.tensor_copy(
-                    out=dealt[:, t0 * P:t1 * P].rearrange("p (t m) -> p t m", m=P),
-                    in_=plane[:, 1, :].bitcast(U8).rearrange("p (m t) -> p t m", t=PACK)[:, t0:t1, :],
-                )
+        spread(xo_scale_table, xo_stage, 64, (1, 0))
+        spread(xt_scale_table, xt_stage, 0, (0, 1))
+        gather(xt_bytes[:], xt_scale_table, tok_list, 0, J)
+        gather(xt_codes[0][:], xt_table, tok_list, 0, HALF)
+        gather(xo_bytes[:], xo_scale_table, note_list, 0, J)
+        gather(xo_codes[0][:], xo_table, note_list, 0, HALF)
+        nc.vector.tensor_copy(out=w_plane[0:64, 1, :], in_=w_plane[64:P, 0, :])
+        w_scale_plane = w_plane[:, 1, :].bitcast(U8)
+        deal_bytes(w_bytes[0], w_scale_plane, 0, 1)
+        w2_plane = sbuf("w2_plane", [P, R], U8)
+        spread(w2_plane, w2_stage, 0, (0, 1))
+        deal_bytes(w2_bytes[0], w2_plane[:], 0, 1)
 
         hidden = [sbuf(f"hidden{t}", [P, J], F32) for t in range(PACK)]
 
-        def first_product(t, first, count, copy):
-            acc = psum.tile([P, count], F32, name=f"acc{t}_{first}")
+        def first_product(acc, t, h):
             rows = slice(t * P, (t + 1) * P)
-            cols = slice(first, first + count)
+            cols = slice(h * HALF, (h + 1) * HALF)
+
+            def scale_columns(dealt):
+                return dealt[0][:] if t == 0 else dealt[1][:, (t - 1) * P:t * P]
+
             nc.tensor.matmul_mx(
-                acc[:], lhsT=w_dealt[:, rows].bitcast(FP4X4), lhsT_scale=w_bytes[:, rows],
-                rhs=xt_codes[:, cols].bitcast(FP8X4), rhs_scale=xt_bytes[:, cols], start=True, stop=False,
+                acc, lhsT=w2_dealt[:, rows].bitcast(FP8X4), lhsT_scale=scale_columns(w2_bytes),
+                rhs=xo_codes[h][:].bitcast(FP4X4), rhs_scale=xo_bytes[:, cols], start=True, stop=False,
             )
             nc.tensor.matmul_mx(
-                acc[:], lhsT=w2_dealt[:, rows].bitcast(FP8X4), lhsT_scale=w2_bytes[:, rows],
-                rhs=xo_codes[:, cols].bitcast(FP4X4), rhs_scale=xo_bytes[:, cols], start=False, stop=True,
+                acc, lhsT=w_dealt[:, rows].bitcast(FP4X4), lhsT_scale=scale_columns(w_bytes),
+                rhs=xt_codes[h][:].bitcast(FP8X4), rhs_scale=xt_bytes[:, cols], start=False, stop=True,
             )
-            copy(out=hidden[t][:, cols], in_=acc[:])
 
         def put_fine(t, first, count):
             nc.scalar.activation(
                 fine[t % 2][:].indirect(entries(fine_list, first, count)), hidden[t][:, first:first + count], COPY
             )
 
-        deal_bytes(0, 1)
-        gather(xo_codes, xo_table, note_list, 0, HALF)
-        first_product(0, 0, HALF, nc.scalar.copy)
+        acc = psum.tile([P, HALF], F32, name="acc0_first")
+        first_product(acc[:], 0, 0)
+        nc.scalar.copy(out=hidden[0][:, 0:HALF], in_=acc[:])
         put_fine(0, 0, HALF)
-        gather(xt_codes, xt_table, tok_list, HALF, HALF)
-        gather(xo_codes, xo_table, note_list, HALF, HALF)
-        first_product(0, HALF, HALF, nc.vector.tensor_copy)
-        deal_bytes(1, PACK)
+        gather(xt_codes[1][:], xt_table, tok_list, HALF, HALF)
+        gather(xo_codes[1][:], xo_table, note_list, HALF, HALF)
+        acc = psum.tile([P, HALF], F32, name="acc0_second")
+        first_product(acc[:], 0, 1)
+        nc.vector.tensor_copy(out=hidden[0][:, HALF:J], in_=acc[:])
+        deal_bytes(w_bytes[1], w_scale_plane, 1, PACK)
+        deal_bytes(w2_bytes[1], w2_plane[:], 1, PACK)
         for t in range(1, PACK):
-            first_product(t, 0, J, nc.vector.tensor_copy)
+            acc = psum.tile([P, J], F32, name=f"acc{t}")
+            for h in range(2):
+                first_product(acc[:, h * HALF:(h + 1) * HALF], t, h)
+            nc.vector.tensor_copy(out=hidden[t][:], in_=acc[:])
 
         vs_codes = sbuf("vs_codes", [P, N], U32)
         vs_bytes = sbuf("vs_bytes", [P, N], U8)
         vs_scale_table = sbuf("vs_scale_table", [P, V], U8)
-        for a in range(2):
-            spread(vs_scale_table, vs_stage, a)
-        gather(vs_bytes, vs_scale_table, store_list, 0, N)
-        gather(vs_codes, vs_table, store_list, 0, N)
+        spread(vs_scale_table, vs_stage, 0, (0, 1))
+        gather(vs_bytes[:], vs_scale_table, store_list, 0, N)
+        gather(vs_codes[:], vs_table, store_list, 0, N)
 
         larger = [sbuf(f"larger{t}", [P, C], F32) for t in range(PACK)]
         picked = [sbuf(f"picked{t}", [P, S], F32) for t in range(PACK)]
@@ -197,16 +216,22 @@ def tile_picked_tokens_plain_bank_coarsefine_store_plain_kernel(
             )
 
         out_rows = out.rearrange("(b p) o -> p b o", p=P)
+        planes = sbuf("planes", [P, PACK, O], BF16)
+
+        def read_board(t, first, count):
+            nc.scalar.activation(
+                planes[:, t, first:first + count], larger[t][:].indirect(entries(read_list, first, count)), COPY,
+                scale=sb_cols[:, t:t + 1],
+            )
+
+        for t in range(2):
+            read_board(t, 0, O)
         for h in range(2):
             cols = slice(h * HALF, (h + 1) * HALF)
-            planes = sbuf(f"planes{h}", [P, PACK, HALF], BF16)
-            for t in range(PACK):
-                nc.scalar.activation(
-                    planes[:, t, :], larger[t][:].indirect(entries(read_list, h * HALF, HALF)), COPY,
-                    scale=sb_cols[:, t:t + 1],
-                )
+            for t in range(2, PACK):
+                read_board(t, h * HALF, HALF)
             woven = sbuf(f"woven{h}", [P, HALF, PACK], BF16)
-            nc.vector.tensor_copy(out=woven[:], in_=planes[:].rearrange("p t o -> p o t"))
+            nc.vector.tensor_copy(out=woven[:], in_=planes[:, :, cols].rearrange("p t o -> p o t"))
             hid_codes = sbuf(f"hid_codes{h}", [P, HALF], U32)
             hid_bytes = sbuf(f"hid_bytes{h}", [P, HALF], U8)
             nc.vector.quantize_mx(

@@ -32,8 +32,8 @@ def tile_picked_tokens_plain_bank_coarsefine_store_plain_kernel(
         reused = ctx.enter_context(tc.tile_pool(name="reused", bufs=1))
         psum = ctx.enter_context(tc.psum_pool(name="psum", bufs=1))
 
-        def sbuf(name, shape, dtype):
-            return keep.tile(shape, dtype, name=name, align_bytes=64)
+        def sbuf(name, shape, dtype, tag=None):
+            return keep.tile(shape, dtype, name=name, tag=tag or name, align_bytes=64)
 
         def load_list(name, src):
             lst = keep.tile(list(src.shape), U16, name=name)
@@ -61,12 +61,12 @@ def tile_picked_tokens_plain_bank_coarsefine_store_plain_kernel(
         xt_stage = sbuf("xt_stage", [64, 2, T // 4], I32)
         xo_stage = sbuf("xo_stage", [P, 2, M // 4], I32)
         w_plane = sbuf("w_plane", [P, 2, R // 4], I32)
-        w2_stage = on_reused_bytes("w2_stage", [64, 2, R // 4], I32, 320)
+        w2_plane = sbuf("w2_plane", [P, 2, R // 4], I32)
         vs_stage = sbuf("vs_stage", [64, 2, V // 4], I32)
         nc.vector.memset(xt_stage[:], 0)
-        nc.gpsimd.memset(xo_stage[64:P], 0)
+        nc.vector.memset(xo_stage[64:P], 0)
         nc.vector.memset(w_plane[64:P], 0)
-        nc.vector.memset(w2_stage[:], 0)
+        nc.vector.memset(w2_plane[64:P], 0)
         nc.vector.memset(vs_stage[:], 0)
 
         def load_columns(name, src):
@@ -77,15 +77,14 @@ def tile_picked_tokens_plain_bank_coarsefine_store_plain_kernel(
         tok_list = load_list("tok_list", offs)
         w_raw = load_words(nc.sync, "w_raw", w_words[0], R, U16)
         for b in range(2):
-            load_scale_rows(nc.scalar, xo_stage, 64, xo_scales, b)
             load_scale_rows(nc.sync, xt_stage, 0, xt_scales, b)
+            load_scale_rows(nc.scalar, xo_stage, 64, xo_scales, b)
         xt_table = load_words(nc.sync, "xt_table", e4m3_rows(xt_words), T, U32)
         xo_table = load_words(nc.sync, "xo_table", xo_words[0], M, U16)
+        for plane, src in ((w_plane, w_scales), (w2_plane, w2_scales)):
+            for b in range(2):
+                load_scale_rows(nc.sync, plane, 64, src, b)
         note_list = load_list("note_list", offs2)
-        for b in range(2):
-            load_scale_rows(nc.sync, w_plane, 64, w_scales, b)
-        for b in range(2):
-            load_scale_rows(nc.sync, w2_stage, 0, w2_scales, b)
         w2_raw = load_words(nc.sync, "w2_raw", e4m3_rows(w2_words), R, U32)
         fine_list = load_list("fine_list", offs3)
         pick_list = load_list("pick_list", offs4)
@@ -99,10 +98,8 @@ def tile_picked_tokens_plain_bank_coarsefine_store_plain_kernel(
         read_list = load_list("read_list", offs6)
 
         fine = [sbuf(f"fine{i}", [P, C], F32) for i in range(2)]
-        coarse = [sbuf(f"coarse{i}", [P, U], F32) for i in range(2)]
-        for i in range(2):
-            nc.vector.memset(fine[i][:], 0.0)
-            nc.vector.memset(coarse[i][:], 0.0)
+        for board in fine:
+            nc.vector.memset(board[:], 0.0)
 
         w_dealt = sbuf("w_dealt", [P, R], U16)
         w2_dealt = sbuf("w2_dealt", [P, R], U32)
@@ -126,47 +123,41 @@ def tile_picked_tokens_plain_bank_coarsefine_store_plain_kernel(
 
         def deal_bytes(dealt, plane, t0, t1):
             nc.vector.tensor_copy(
-                out=dealt[:].rearrange("p (t m) -> p t m", m=P),
-                in_=plane.rearrange("p (m t) -> p t m", t=PACK)[:, t0:t1, :],
+                out=dealt[:].rearrange("p (t m) -> p t m", m=P)[:, t0:t1, :],
+                in_=plane[:, 1, :].bitcast(U8).rearrange("p (m t) -> p t m", t=PACK)[:, t0:t1, :],
             )
 
-        xt_codes = [sbuf("xt_codes0", [P, HALF], U32), on_reused_bytes("xt_codes1", [P, HALF], U32, 384)]
-        xo_codes = [sbuf("xo_codes0", [P, HALF], U16), on_reused_bytes("xo_codes1", [P, HALF], U16, 896)]
+        xo_scale_table = on_reused_bytes("xo_scale_table", [P, M], U8, 448)
+        w2_bytes = on_reused_bytes("w2_bytes", [P, R], U8, 0)
+        xo_codes = [sbuf("xo_codes0", [P, HALF], U16), on_reused_bytes("xo_codes1", [P, HALF], U16, 512)]
+        w_bytes = on_reused_bytes("w_bytes", [P, R], U8, 768)
+        xt_codes = [sbuf("xt_codes0", [P, HALF], U32), on_reused_bytes("xt_codes1", [P, HALF], U32, 1280)]
         xt_bytes = sbuf("xt_bytes", [P, J], U8)
         xo_bytes = sbuf("xo_bytes", [P, J], U8)
-        w_bytes = [sbuf("w_bytes0", [P, P], U8), on_reused_bytes("w_bytes1", [P, R - P], U8, 1152)]
-        w2_bytes = [sbuf("w2_bytes0", [P, P], U8), on_reused_bytes("w2_bytes1", [P, R - P], U8, 0)]
 
         xt_scale_table = sbuf("xt_scale_table", [P, T], U8)
-        xo_scale_table = sbuf("xo_scale_table", [P, M], U8)
-        spread(xo_scale_table, xo_stage, 64, (1, 0))
         spread(xt_scale_table, xt_stage, 0, (0, 1))
+        spread(xo_scale_table, xo_stage, 64, (1, 0))
         gather(xt_bytes[:], xt_scale_table, tok_list, 0, J)
         gather(xt_codes[0][:], xt_table, tok_list, 0, HALF)
+        for plane in (w_plane, w2_plane):
+            nc.vector.tensor_copy(out=plane[0:64, 1, :], in_=plane[64:P, 0, :])
         gather(xo_bytes[:], xo_scale_table, note_list, 0, J)
         gather(xo_codes[0][:], xo_table, note_list, 0, HALF)
-        nc.vector.tensor_copy(out=w_plane[0:64, 1, :], in_=w_plane[64:P, 0, :])
-        w_scale_plane = w_plane[:, 1, :].bitcast(U8)
-        deal_bytes(w_bytes[0], w_scale_plane, 0, 1)
-        w2_plane = sbuf("w2_plane", [P, R], U8)
-        spread(w2_plane, w2_stage, 0, (0, 1))
-        deal_bytes(w2_bytes[0], w2_plane[:], 0, 1)
+        deal_bytes(w2_bytes, w2_plane, 0, 1)
+        deal_bytes(w_bytes, w_plane, 0, 1)
 
         hidden = [sbuf(f"hidden{t}", [P, J], F32) for t in range(PACK)]
 
         def first_product(acc, t, h):
             rows = slice(t * P, (t + 1) * P)
             cols = slice(h * HALF, (h + 1) * HALF)
-
-            def scale_columns(dealt):
-                return dealt[0][:] if t == 0 else dealt[1][:, (t - 1) * P:t * P]
-
             nc.tensor.matmul_mx(
-                acc, lhsT=w2_dealt[:, rows].bitcast(FP8X4), lhsT_scale=scale_columns(w2_bytes),
+                acc, lhsT=w2_dealt[:, rows].bitcast(FP8X4), lhsT_scale=w2_bytes[:, rows],
                 rhs=xo_codes[h][:].bitcast(FP4X4), rhs_scale=xo_bytes[:, cols], start=True, stop=False,
             )
             nc.tensor.matmul_mx(
-                acc, lhsT=w_dealt[:, rows].bitcast(FP4X4), lhsT_scale=scale_columns(w_bytes),
+                acc, lhsT=w_dealt[:, rows].bitcast(FP4X4), lhsT_scale=w_bytes[:, rows],
                 rhs=xt_codes[h][:].bitcast(FP8X4), rhs_scale=xt_bytes[:, cols], start=False, stop=True,
             )
 
@@ -184,13 +175,20 @@ def tile_picked_tokens_plain_bank_coarsefine_store_plain_kernel(
         acc = psum.tile([P, HALF], F32, name="acc0_second")
         first_product(acc[:], 0, 1)
         nc.vector.tensor_copy(out=hidden[0][:, HALF:J], in_=acc[:])
-        deal_bytes(w_bytes[1], w_scale_plane, 1, PACK)
-        deal_bytes(w2_bytes[1], w2_plane[:], 1, PACK)
+        deal_bytes(w2_bytes, w2_plane, 1, PACK)
+        deal_bytes(w_bytes, w_plane, 1, PACK)
         for t in range(1, PACK):
             acc = psum.tile([P, J], F32, name=f"acc{t}")
             for h in range(2):
                 first_product(acc[:, h * HALF:(h + 1) * HALF], t, h)
             nc.vector.tensor_copy(out=hidden[t][:], in_=acc[:])
+
+        coarse = [
+            sbuf(f"coarse{t}", [P, U], F32, tag=tag)
+            for t, tag in enumerate(("w2_plane", "w_plane", "xo_codes0", "xt_codes0"))
+        ]
+        for board in coarse:
+            nc.gpsimd.memset(board[:], 0.0)
 
         vs_codes = sbuf("vs_codes", [P, N], U32)
         vs_bytes = sbuf("vs_bytes", [P, N], U8)
@@ -207,11 +205,11 @@ def tile_picked_tokens_plain_bank_coarsefine_store_plain_kernel(
                 put_fine(t, HALF, HALF)
             else:
                 put_fine(t, 0, J)
-            nc.scalar.activation(coarse[t % 2][:].indirect(coarse_list[:]), picked[t][:], COPY)
+            nc.scalar.activation(coarse[t][:].indirect(coarse_list[:]), picked[t][:], COPY)
             nc.vector.tensor_tensor(
                 out=larger[t][:].rearrange("p (u e) -> p u e", e=C // U),
                 in0=fine[t % 2][:].rearrange("p (u e) -> p u e", e=C // U),
-                in1=coarse[t % 2][:].unsqueeze(2).to_broadcast([P, U, C // U]),
+                in1=coarse[t][:].unsqueeze(2).to_broadcast([P, U, C // U]),
                 op=MAX,
             )
 

@@ -48,9 +48,13 @@ def tile_picked_tokens_plain_bank_coarsefine_store_plain_kernel(
             queue.dma_start(out=words[:].bitcast(I32), in_=src.bitcast(I32))
             return words
 
-        def load_scale_rows(queue, stage, base, src, b):
+        def load_plane_rows(plane, src, b):
             rows = src[0].bitcast(I32).rearrange("(a b j) n -> b j a n", a=2, b=2)
-            queue.dma_start(out=stage[base + 32 * b:base + 32 * b + 4, :, :], in_=rows[b])
+            nc.sync.dma_start(out=plane[64 + 32 * b:64 + 32 * b + 4, :, :], in_=rows[b])
+
+        def load_stage_rows(queue, stage, src, a):
+            rows = src[0].bitcast(I32).rearrange("(a b j) n -> a j b n", a=2, b=2)
+            queue.dma_start(out=stage[64 * a:64 * a + 4, :, :], in_=rows[a])
 
         def e4m3_rows(src):
             return src[0].rearrange("p n t -> p (n t)")
@@ -58,39 +62,40 @@ def tile_picked_tokens_plain_bank_coarsefine_store_plain_kernel(
         def on_reused_bytes(name, shape, dtype, offset):
             return reused.tile(shape, dtype, name=name, align_bytes=64, offset=offset)
 
-        xt_stage = sbuf("xt_stage", [64, 2, T // 4], I32)
+        xt_stage = sbuf("xt_stage", [P, 2, T // 4], I32)
         xo_stage = sbuf("xo_stage", [P, 2, M // 4], I32)
+        vs_stage = sbuf("vs_stage", [P, 2, V // 4], I32)
         w_plane = sbuf("w_plane", [P, 2, R // 4], I32)
         w2_plane = sbuf("w2_plane", [P, 2, R // 4], I32)
-        vs_stage = sbuf("vs_stage", [64, 2, V // 4], I32)
-        nc.vector.memset(xt_stage[:], 0)
-        nc.vector.memset(xo_stage[64:P], 0)
+        xt_scale_table = sbuf("xt_scale_table", [P, T], U8)
+        xo_scale_table = on_reused_bytes("xo_scale_table", [P, M], U8, 448)
         nc.vector.memset(w_plane[64:P], 0)
         nc.vector.memset(w2_plane[64:P], 0)
-        nc.vector.memset(vs_stage[:], 0)
+        nc.vector.memset(xt_scale_table[:].bitcast(I32), 0)
+        nc.vector.memset(xo_scale_table[:].bitcast(I32), 0)
 
         def load_columns(name, src):
             cols = sbuf(name, [P, PACK], F32)
             nc.sync.dma_start(out=cols[:], in_=src.rearrange("(p t) o -> p (t o)", t=PACK))
             return cols
 
+        for a in range(2):
+            load_stage_rows(nc.sync, xt_stage, xt_scales, a)
+            load_stage_rows(nc.scalar, xo_stage, xo_scales, a)
         tok_list = load_list("tok_list", offs)
-        w_raw = load_words(nc.sync, "w_raw", w_words[0], R, U16)
-        for b in range(2):
-            load_scale_rows(nc.sync, xt_stage, 0, xt_scales, b)
-            load_scale_rows(nc.scalar, xo_stage, 64, xo_scales, b)
+        w_raw = load_words(nc.scalar, "w_raw", w_words[0], R, U16)
         xt_table = load_words(nc.sync, "xt_table", e4m3_rows(xt_words), T, U32)
-        xo_table = load_words(nc.sync, "xo_table", xo_words[0], M, U16)
+        xo_table = load_words(nc.scalar, "xo_table", xo_words[0], M, U16)
         for plane, src in ((w_plane, w_scales), (w2_plane, w2_scales)):
             for b in range(2):
-                load_scale_rows(nc.sync, plane, 64, src, b)
+                load_plane_rows(plane, src, b)
         note_list = load_list("note_list", offs2)
         w2_raw = load_words(nc.sync, "w2_raw", e4m3_rows(w2_words), R, U32)
         fine_list = load_list("fine_list", offs3)
         pick_list = load_list("pick_list", offs4)
         sa_cols = load_columns("sa_cols", sa)
-        for b in range(2):
-            load_scale_rows(nc.sync, vs_stage, 0, vs_scales, b)
+        for a in range(2):
+            load_stage_rows(nc.sync, vs_stage, vs_scales, a)
         store_list = load_list("store_list", offs7)
         vs_table = load_words(nc.sync, "vs_table", e4m3_rows(vs_words), V, U32)
         coarse_list = load_list("coarse_list", offs5)
@@ -114,9 +119,13 @@ def tile_picked_tokens_plain_bank_coarsefine_store_plain_kernel(
         deal_words(w2_dealt, w2_raw, 0, 1)
         deal_words(w2_dealt, w2_raw, 1, PACK)
 
-        def spread(plane, stage, base, halves):
-            for a in halves:
-                nc.vector.tensor_copy(out=plane[64 * a:64 * a + 64, :].bitcast(I32), in_=stage[base:base + 64, a, :])
+        def spread(pairs):
+            for q in range(4):
+                a, b = divmod(q, 2)
+                for table, stage in pairs:
+                    nc.vector.tensor_copy(
+                        out=table[32 * q:32 * q + 4, :].bitcast(I32), in_=stage[64 * a:64 * a + 4, b, :]
+                    )
 
         def gather(dst, table, lst, first, count):
             nc.vector.tensor_copy(dst, table[:].indirect(entries(lst, first, count)))
@@ -127,7 +136,6 @@ def tile_picked_tokens_plain_bank_coarsefine_store_plain_kernel(
                 in_=plane[:, 1, :].bitcast(U8).rearrange("p (m t) -> p t m", t=PACK)[:, t0:t1, :],
             )
 
-        xo_scale_table = on_reused_bytes("xo_scale_table", [P, M], U8, 448)
         w2_bytes = on_reused_bytes("w2_bytes", [P, R], U8, 0)
         xo_codes = [sbuf("xo_codes0", [P, HALF], U16), on_reused_bytes("xo_codes1", [P, HALF], U16, 512)]
         w_bytes = on_reused_bytes("w_bytes", [P, R], U8, 768)
@@ -135,9 +143,7 @@ def tile_picked_tokens_plain_bank_coarsefine_store_plain_kernel(
         xt_bytes = sbuf("xt_bytes", [P, J], U8)
         xo_bytes = sbuf("xo_bytes", [P, J], U8)
 
-        xt_scale_table = sbuf("xt_scale_table", [P, T], U8)
-        spread(xt_scale_table, xt_stage, 0, (0, 1))
-        spread(xo_scale_table, xo_stage, 64, (1, 0))
+        spread(((xt_scale_table, xt_stage), (xo_scale_table, xo_stage)))
         gather(xt_bytes[:], xt_scale_table, tok_list, 0, J)
         gather(xt_codes[0][:], xt_table, tok_list, 0, HALF)
         for plane in (w_plane, w2_plane):
@@ -183,17 +189,18 @@ def tile_picked_tokens_plain_bank_coarsefine_store_plain_kernel(
                 first_product(acc[:, h * HALF:(h + 1) * HALF], t, h)
             nc.vector.tensor_copy(out=hidden[t][:], in_=acc[:])
 
+        vs_scale_table = sbuf("vs_scale_table", [P, V], U8, tag="w_dealt")
+        nc.gpsimd.memset(vs_scale_table[:].bitcast(I32), 0)
         coarse = [
             sbuf(f"coarse{t}", [P, U], F32, tag=tag)
-            for t, tag in enumerate(("w2_plane", "w_plane", "xo_codes0", "xt_codes0"))
+            for t, tag in enumerate(("xo_codes0", "xt_codes0", "xo_bytes", "xt_bytes"))
         ]
         for board in coarse:
             nc.gpsimd.memset(board[:], 0.0)
 
         vs_codes = sbuf("vs_codes", [P, N], U32)
         vs_bytes = sbuf("vs_bytes", [P, N], U8)
-        vs_scale_table = sbuf("vs_scale_table", [P, V], U8)
-        spread(vs_scale_table, vs_stage, 0, (0, 1))
+        spread(((vs_scale_table, vs_stage),))
         gather(vs_bytes[:], vs_scale_table, store_list, 0, N)
         gather(vs_codes[:], vs_table, store_list, 0, N)
 

@@ -20,6 +20,11 @@ P = 128
 PACK = 4
 HALF = 128
 LIST_ROWS = 16
+QUADRANT = 32
+SCALE_ROWS = 4
+UPPER = 64
+ALIGN = 64
+FINE_BOARDS = 2
 
 
 def tile_picked_tokens_plain_bank_coarsefine_store_plain_kernel(
@@ -33,7 +38,7 @@ def tile_picked_tokens_plain_bank_coarsefine_store_plain_kernel(
         psum = ctx.enter_context(tc.psum_pool(name="psum", bufs=1))
 
         def sbuf(name, shape, dtype, tag=None):
-            return keep.tile(shape, dtype, name=name, tag=tag or name, align_bytes=64)
+            return keep.tile(shape, dtype, name=name, tag=tag or name, align_bytes=ALIGN)
 
         def load_list(name, src):
             lst = keep.tile(list(src.shape), U16, name=name)
@@ -48,29 +53,30 @@ def tile_picked_tokens_plain_bank_coarsefine_store_plain_kernel(
             queue.dma_start(out=words[:].bitcast(I32), in_=src.bitcast(I32))
             return words
 
-        def load_plane_rows(plane, src, b):
+        def load_plane_rows(paired, src, b):
             rows = src[0].bitcast(I32).rearrange("(a b j) n -> b j a n", a=2, b=2)
-            nc.sync.dma_start(out=plane[64 + 32 * b:64 + 32 * b + 4, :, :], in_=rows[b])
+            first = UPPER + QUADRANT * b
+            nc.sync.dma_start(out=paired[first:first + SCALE_ROWS, :, :], in_=rows[b])
 
         def load_stage_rows(queue, stage, src, a):
             rows = src[0].bitcast(I32).rearrange("(a b j) n -> a j b n", a=2, b=2)
-            queue.dma_start(out=stage[64 * a:64 * a + 4, :, :], in_=rows[a])
+            queue.dma_start(out=stage[UPPER * a:UPPER * a + SCALE_ROWS, :, :], in_=rows[a])
 
         def e4m3_rows(src):
             return src[0].rearrange("p n t -> p (n t)")
 
         def on_reused_bytes(name, shape, dtype, offset):
-            return reused.tile(shape, dtype, name=name, align_bytes=64, offset=offset)
+            return reused.tile(shape, dtype, name=name, align_bytes=ALIGN, offset=offset)
 
         xt_stage = sbuf("xt_stage", [P, 2, T // 4], I32)
         xo_stage = sbuf("xo_stage", [P, 2, M // 4], I32)
         vs_stage = sbuf("vs_stage", [P, 2, V // 4], I32)
-        w_plane = sbuf("w_plane", [P, 2, R // 4], I32)
-        w2_plane = sbuf("w2_plane", [P, 2, R // 4], I32)
+        w_paired = sbuf("w_paired", [P, 2, R // 4], I32)
+        w2_paired = sbuf("w2_paired", [P, 2, R // 4], I32)
         xt_scale_table = sbuf("xt_scale_table", [P, T], U8)
-        xo_scale_table = on_reused_bytes("xo_scale_table", [P, M], U8, 448)
-        nc.vector.memset(w_plane[64:P], 0)
-        nc.vector.memset(w2_plane[64:P], 0)
+        xo_scale_table = on_reused_bytes("xo_scale_table", [P, M], U8, R - ALIGN)
+        nc.vector.memset(w_paired[UPPER:P], 0)
+        nc.vector.memset(w2_paired[UPPER:P], 0)
         nc.vector.memset(xt_scale_table[:].bitcast(I32), 0)
         nc.vector.memset(xo_scale_table[:].bitcast(I32), 0)
 
@@ -79,16 +85,16 @@ def tile_picked_tokens_plain_bank_coarsefine_store_plain_kernel(
             nc.sync.dma_start(out=cols[:], in_=src.rearrange("(p t) o -> p (t o)", t=PACK))
             return cols
 
-        for a in range(2):
+        for a in (1, 0):
             load_stage_rows(nc.sync, xt_stage, xt_scales, a)
             load_stage_rows(nc.scalar, xo_stage, xo_scales, a)
         tok_list = load_list("tok_list", offs)
         w_raw = load_words(nc.scalar, "w_raw", w_words[0], R, U16)
         xt_table = load_words(nc.sync, "xt_table", e4m3_rows(xt_words), T, U32)
         xo_table = load_words(nc.scalar, "xo_table", xo_words[0], M, U16)
-        for plane, src in ((w_plane, w_scales), (w2_plane, w2_scales)):
+        for paired, src in ((w_paired, w_scales), (w2_paired, w2_scales)):
             for b in range(2):
-                load_plane_rows(plane, src, b)
+                load_plane_rows(paired, src, b)
         note_list = load_list("note_list", offs2)
         w2_raw = load_words(nc.sync, "w2_raw", e4m3_rows(w2_words), R, U32)
         fine_list = load_list("fine_list", offs3)
@@ -102,7 +108,7 @@ def tile_picked_tokens_plain_bank_coarsefine_store_plain_kernel(
         sb_cols = load_columns("sb_cols", sb)
         read_list = load_list("read_list", offs6)
 
-        fine = [sbuf(f"fine{i}", [P, C], F32) for i in range(2)]
+        fine = [sbuf(f"fine{i}", [P, C], F32) for i in range(FINE_BOARDS)]
         for board in fine:
             nc.vector.memset(board[:], 0.0)
 
@@ -120,38 +126,39 @@ def tile_picked_tokens_plain_bank_coarsefine_store_plain_kernel(
         deal_words(w2_dealt, w2_raw, 1, PACK)
 
         def spread(pairs):
-            for q in range(4):
+            for q in (2, 3, 1, 0):
                 a, b = divmod(q, 2)
                 for table, stage in pairs:
                     nc.vector.tensor_copy(
-                        out=table[32 * q:32 * q + 4, :].bitcast(I32), in_=stage[64 * a:64 * a + 4, b, :]
+                        out=table[QUADRANT * q:QUADRANT * q + SCALE_ROWS, :].bitcast(I32),
+                        in_=stage[UPPER * a:UPPER * a + SCALE_ROWS, b, :],
                     )
 
         def gather(dst, table, lst, first, count):
             nc.vector.tensor_copy(dst, table[:].indirect(entries(lst, first, count)))
 
-        def deal_bytes(dealt, plane, t0, t1):
+        def deal_bytes(dealt, paired, t0, t1):
             nc.vector.tensor_copy(
                 out=dealt[:].rearrange("p (t m) -> p t m", m=P)[:, t0:t1, :],
-                in_=plane[:, 1, :].bitcast(U8).rearrange("p (m t) -> p t m", t=PACK)[:, t0:t1, :],
+                in_=paired[:, 1, :].bitcast(U8).rearrange("p (m t) -> p t m", t=PACK)[:, t0:t1, :],
             )
 
         w2_bytes = on_reused_bytes("w2_bytes", [P, R], U8, 0)
-        xo_codes = [sbuf("xo_codes0", [P, HALF], U16), on_reused_bytes("xo_codes1", [P, HALF], U16, 512)]
-        w_bytes = on_reused_bytes("w_bytes", [P, R], U8, 768)
-        xt_codes = [sbuf("xt_codes0", [P, HALF], U32), on_reused_bytes("xt_codes1", [P, HALF], U32, 1280)]
-        xt_bytes = sbuf("xt_bytes", [P, J], U8)
+        xo_codes = [sbuf("xo_codes0", [P, HALF], U16), on_reused_bytes("xo_codes1", [P, HALF], U16, R)]
+        w_bytes = on_reused_bytes("w_bytes", [P, R], U8, R + 2 * HALF)
+        xt_codes = [sbuf("xt_codes0", [P, HALF], U32), on_reused_bytes("xt_codes1", [P, HALF], U32, 2 * R + 3 * HALF)]
+        xt_bytes = [sbuf("xt_bytes0", [P, HALF], U8), on_reused_bytes("xt_bytes1", [P, HALF], U8, 2 * R + 2 * HALF)]
         xo_bytes = sbuf("xo_bytes", [P, J], U8)
 
         spread(((xt_scale_table, xt_stage), (xo_scale_table, xo_stage)))
-        gather(xt_bytes[:], xt_scale_table, tok_list, 0, J)
+        gather(xt_bytes[0][:], xt_scale_table, tok_list, 0, HALF)
         gather(xt_codes[0][:], xt_table, tok_list, 0, HALF)
-        for plane in (w_plane, w2_plane):
-            nc.vector.tensor_copy(out=plane[0:64, 1, :], in_=plane[64:P, 0, :])
+        for paired in (w_paired, w2_paired):
+            nc.vector.tensor_copy(out=paired[0:UPPER, 1, :], in_=paired[UPPER:P, 0, :])
         gather(xo_bytes[:], xo_scale_table, note_list, 0, J)
         gather(xo_codes[0][:], xo_table, note_list, 0, HALF)
-        deal_bytes(w2_bytes, w2_plane, 0, 1)
-        deal_bytes(w_bytes, w_plane, 0, 1)
+        deal_bytes(w2_bytes, w2_paired, 0, 1)
+        deal_bytes(w_bytes, w_paired, 0, 1)
 
         hidden = [sbuf(f"hidden{t}", [P, J], F32) for t in range(PACK)]
 
@@ -164,25 +171,27 @@ def tile_picked_tokens_plain_bank_coarsefine_store_plain_kernel(
             )
             nc.tensor.matmul_mx(
                 acc, lhsT=w_dealt[:, rows].bitcast(FP4X4), lhsT_scale=w_bytes[:, rows],
-                rhs=xt_codes[h][:].bitcast(FP8X4), rhs_scale=xt_bytes[:, cols], start=False, stop=True,
+                rhs=xt_codes[h][:].bitcast(FP8X4), rhs_scale=xt_bytes[h][:], start=False, stop=True,
             )
 
         def put_fine(t, first, count):
             nc.scalar.activation(
-                fine[t % 2][:].indirect(entries(fine_list, first, count)), hidden[t][:, first:first + count], COPY
+                fine[t % FINE_BOARDS][:].indirect(entries(fine_list, first, count)),
+                hidden[t][:, first:first + count], COPY,
             )
 
         acc = psum.tile([P, HALF], F32, name="acc0_first")
         first_product(acc[:], 0, 0)
         nc.scalar.copy(out=hidden[0][:, 0:HALF], in_=acc[:])
         put_fine(0, 0, HALF)
-        gather(xt_codes[1][:], xt_table, tok_list, HALF, HALF)
         gather(xo_codes[1][:], xo_table, note_list, HALF, HALF)
+        gather(xt_bytes[1][:], xt_scale_table, tok_list, HALF, HALF)
+        gather(xt_codes[1][:], xt_table, tok_list, HALF, HALF)
         acc = psum.tile([P, HALF], F32, name="acc0_second")
         first_product(acc[:], 0, 1)
         nc.vector.tensor_copy(out=hidden[0][:, HALF:J], in_=acc[:])
-        deal_bytes(w2_bytes, w2_plane, 1, PACK)
-        deal_bytes(w_bytes, w_plane, 1, PACK)
+        deal_bytes(w2_bytes, w2_paired, 1, PACK)
+        deal_bytes(w_bytes, w_paired, 1, PACK)
         for t in range(1, PACK):
             acc = psum.tile([P, J], F32, name=f"acc{t}")
             for h in range(2):
@@ -193,7 +202,7 @@ def tile_picked_tokens_plain_bank_coarsefine_store_plain_kernel(
         nc.gpsimd.memset(vs_scale_table[:].bitcast(I32), 0)
         coarse = [
             sbuf(f"coarse{t}", [P, U], F32, tag=tag)
-            for t, tag in enumerate(("xo_codes0", "xt_codes0", "xo_bytes", "xt_bytes"))
+            for t, tag in enumerate(("xo_codes0", "xt_codes0", "xo_bytes", "xt_bytes0"))
         ]
         for board in coarse:
             nc.gpsimd.memset(board[:], 0.0)
@@ -208,39 +217,43 @@ def tile_picked_tokens_plain_bank_coarsefine_store_plain_kernel(
         picked = [sbuf(f"picked{t}", [P, S], F32) for t in range(PACK)]
         for t in range(PACK):
             nc.scalar.activation(picked[t][:], hidden[t][:].indirect(pick_list[:]), COPY, scale=sa_cols[:, t:t + 1])
-            if t == 0:
-                put_fine(t, HALF, HALF)
-            else:
-                put_fine(t, 0, J)
+            first = HALF if t == 0 else 0
+            put_fine(t, first, J - first)
             nc.scalar.activation(coarse[t][:].indirect(coarse_list[:]), picked[t][:], COPY)
             nc.vector.tensor_tensor(
                 out=larger[t][:].rearrange("p (u e) -> p u e", e=C // U),
-                in0=fine[t % 2][:].rearrange("p (u e) -> p u e", e=C // U),
+                in0=fine[t % FINE_BOARDS][:].rearrange("p (u e) -> p u e", e=C // U),
                 in1=coarse[t][:].unsqueeze(2).to_broadcast([P, U, C // U]),
                 op=MAX,
             )
 
         out_rows = out.rearrange("(b p) o -> p b o", p=P)
-        planes = sbuf("planes", [P, PACK, O], BF16)
+        hid = sbuf("hid", [P, PACK, O], BF16)
 
         def read_board(t, first, count):
             nc.scalar.activation(
-                planes[:, t, first:first + count], larger[t][:].indirect(entries(read_list, first, count)), COPY,
+                hid[:, t, first:first + count], larger[t][:].indirect(entries(read_list, first, count)), COPY,
                 scale=sb_cols[:, t:t + 1],
             )
 
+        woven = sbuf("woven", [P, O, PACK], BF16)
+
+        def weave(tiles, cols):
+            nc.vector.tensor_copy(out=woven[:, cols, tiles], in_=hid[:, tiles, cols].rearrange("p t o -> p o t"))
+
         for t in range(2):
             read_board(t, 0, O)
+        weave(slice(0, 2), slice(0, O))
         for h in range(2):
             cols = slice(h * HALF, (h + 1) * HALF)
             for t in range(2, PACK):
                 read_board(t, h * HALF, HALF)
-            woven = sbuf(f"woven{h}", [P, HALF, PACK], BF16)
-            nc.vector.tensor_copy(out=woven[:], in_=planes[:, :, cols].rearrange("p t o -> p o t"))
+            weave(slice(2, PACK), cols)
             hid_codes = sbuf(f"hid_codes{h}", [P, HALF], U32)
             hid_bytes = sbuf(f"hid_bytes{h}", [P, HALF], U8)
             nc.vector.quantize_mx(
-                out=hid_codes[:].bitcast(FP8X4), scales=hid_bytes[:], in_=woven[:].rearrange("p o t -> p (o t)")
+                out=hid_codes[:].bitcast(FP8X4), scales=hid_bytes[:],
+                in_=woven[:, cols, :].rearrange("p o t -> p (o t)"),
             )
 
             def second_product(acc, b):

from contextlib import ExitStack

import concourse.mybir as mybir

K, J, R, T, Z, M, C, O, S, U, N, V = 512, 256, 512, 1024, 512, 1024, 512, 256, 128, 256, 256, 1024
FLOPS = 2 * (K * R * J + Z * R * J + R * N * O)

F32 = mybir.dt.float32
BF16 = mybir.dt.bfloat16
I32 = mybir.dt.int32
U32 = mybir.dt.uint32
U16 = mybir.dt.uint16
U8 = mybir.dt.uint8
FP8X4 = mybir.dt.float8_e4m3fn_x4
FP4X4 = mybir.dt.float4_e2m1fn_x4
COPY = mybir.ActivationFunctionType.Copy
MAX = mybir.AluOpType.max

P = 128
PACK = 4
HALF = 128
LIST_ROWS = 16
QUADRANT = 32
SCALE_ROWS = 4
UPPER = 64
ALIGN = 64
FINE_BOARDS = 2


def tile_picked_tokens_plain_bank_coarsefine_store_plain_kernel(
    tc, xt_words, xt_scales, w_words, w_scales, xo_words, xo_scales, w2_words, w2_scales, sa, sb,
    vs_words, vs_scales, offs, offs2, offs3, offs4, offs5, offs6, offs7, out,
):
    nc = tc.nc
    with ExitStack() as ctx:
        keep = ctx.enter_context(tc.tile_pool(name="keep", bufs=1))
        reused = ctx.enter_context(tc.tile_pool(name="reused", bufs=1))
        psum = ctx.enter_context(tc.psum_pool(name="psum", bufs=1))

        def sbuf(name, shape, dtype, tag=None):
            return keep.tile(shape, dtype, name=name, tag=tag or name, align_bytes=ALIGN)

        def load_list(name, src):
            lst = keep.tile(list(src.shape), U16, name=name)
            nc.sync.dma_start(lst[:], src)
            return lst

        def entries(lst, first, count):
            return lst[:, first // LIST_ROWS:(first + count) // LIST_ROWS]

        def load_words(queue, name, src, cols, dtype):
            words = sbuf(name, [P, cols], dtype)
            queue.dma_start(out=words[:].bitcast(I32), in_=src.bitcast(I32))
            return words

        def load_plane_rows(paired, src, b):
            rows = src[0].bitcast(I32).rearrange("(a b j) n -> b j a n", a=2, b=2)
            first = UPPER + QUADRANT * b
            nc.sync.dma_start(out=paired[first:first + SCALE_ROWS, :, :], in_=rows[b])

        def load_stage_rows(queue, stage, src, a):
            rows = src[0].bitcast(I32).rearrange("(a b j) n -> a j b n", a=2, b=2)
            queue.dma_start(out=stage[UPPER * a:UPPER * a + SCALE_ROWS, :, :], in_=rows[a])

        def e4m3_rows(src):
            return src[0].rearrange("p n t -> p (n t)")

        def on_reused_bytes(name, shape, dtype, offset):
            return reused.tile(shape, dtype, name=name, align_bytes=ALIGN, offset=offset)

        xt_stage = sbuf("xt_stage", [P, 2, T // 4], I32)
        xo_stage = sbuf("xo_stage", [P, 2, M // 4], I32)
        vs_stage = sbuf("vs_stage", [P, 2, V // 4], I32)
        w_paired = sbuf("w_paired", [P, 2, R // 4], I32)
        w2_paired = sbuf("w2_paired", [P, 2, R // 4], I32)
        xt_scale_table = sbuf("xt_scale_table", [P, T], U8)
        xo_scale_table = on_reused_bytes("xo_scale_table", [P, M], U8, R - ALIGN)
        nc.vector.memset(w_paired[UPPER:P], 0)
        nc.vector.memset(w2_paired[UPPER:P], 0)
        nc.vector.memset(xt_scale_table[:].bitcast(I32), 0)
        nc.vector.memset(xo_scale_table[:].bitcast(I32), 0)

        def load_columns(name, src):
            cols = sbuf(name, [P, PACK], F32)
            nc.sync.dma_start(out=cols[:], in_=src.rearrange("(p t) o -> p (t o)", t=PACK))
            return cols

        for a in (1, 0):
            load_stage_rows(nc.sync, xt_stage, xt_scales, a)
            load_stage_rows(nc.scalar, xo_stage, xo_scales, a)
        tok_list = load_list("tok_list", offs)
        w_raw = load_words(nc.scalar, "w_raw", w_words[0], R, U16)
        xt_table = load_words(nc.sync, "xt_table", e4m3_rows(xt_words), T, U32)
        xo_table = load_words(nc.scalar, "xo_table", xo_words[0], M, U16)
        for paired, src in ((w_paired, w_scales), (w2_paired, w2_scales)):
            for b in range(2):
                load_plane_rows(paired, src, b)
        note_list = load_list("note_list", offs2)
        w2_raw = load_words(nc.sync, "w2_raw", e4m3_rows(w2_words), R, U32)
        fine_list = load_list("fine_list", offs3)
        pick_list = load_list("pick_list", offs4)
        sa_cols = load_columns("sa_cols", sa)
        for a in range(2):
            load_stage_rows(nc.sync, vs_stage, vs_scales, a)
        store_list = load_list("store_list", offs7)
        vs_table = load_words(nc.sync, "vs_table", e4m3_rows(vs_words), V, U32)
        coarse_list = load_list("coarse_list", offs5)
        sb_cols = load_columns("sb_cols", sb)
        read_list = load_list("read_list", offs6)

        fine = [sbuf(f"fine{i}", [P, C], F32) for i in range(FINE_BOARDS)]
        for board in fine:
            nc.vector.memset(board[:], 0.0)

        w_dealt = sbuf("w_dealt", [P, R], U16)
        w2_dealt = sbuf("w2_dealt", [P, R], U32)

        def deal_words(dealt, raw, t0, t1):
            nc.scalar.copy(
                out=dealt[:].rearrange("p (t m) -> p m t", t=PACK)[:, :, t0:t1],
                in_=raw[:].rearrange("p (m t) -> p m t", t=PACK)[:, :, t0:t1],
            )

        deal_words(w_dealt, w_raw, 0, PACK)
        deal_words(w2_dealt, w2_raw, 0, 1)
        deal_words(w2_dealt, w2_raw, 1, PACK)

        def spread(pairs):
            for q in (2, 3, 1, 0):
                a, b = divmod(q, 2)
                for table, stage in pairs:
                    nc.vector.tensor_copy(
                        out=table[QUADRANT * q:QUADRANT * q + SCALE_ROWS, :].bitcast(I32),
                        in_=stage[UPPER * a:UPPER * a + SCALE_ROWS, b, :],
                    )

        def gather(dst, table, lst, first, count):
            nc.vector.tensor_copy(dst, table[:].indirect(entries(lst, first, count)))

        def deal_bytes(dealt, paired, t0, t1):
            nc.vector.tensor_copy(
                out=dealt[:].rearrange("p (t m) -> p t m", m=P)[:, t0:t1, :],
                in_=paired[:, 1, :].bitcast(U8).rearrange("p (m t) -> p t m", t=PACK)[:, t0:t1, :],
            )

        w2_bytes = on_reused_bytes("w2_bytes", [P, R], U8, 0)
        xo_codes = [sbuf("xo_codes0", [P, HALF], U16), on_reused_bytes("xo_codes1", [P, HALF], U16, R)]
        w_bytes = on_reused_bytes("w_bytes", [P, R], U8, R + 2 * HALF)
        xt_codes = [sbuf("xt_codes0", [P, HALF], U32), on_reused_bytes("xt_codes1", [P, HALF], U32, 2 * R + 3 * HALF)]
        xt_bytes = [sbuf("xt_bytes0", [P, HALF], U8), on_reused_bytes("xt_bytes1", [P, HALF], U8, 2 * R + 2 * HALF)]
        xo_bytes = sbuf("xo_bytes", [P, J], U8)

        spread(((xt_scale_table, xt_stage), (xo_scale_table, xo_stage)))
        gather(xt_bytes[0][:], xt_scale_table, tok_list, 0, HALF)
        gather(xt_codes[0][:], xt_table, tok_list, 0, HALF)
        for paired in (w_paired, w2_paired):
            nc.vector.tensor_copy(out=paired[0:UPPER, 1, :], in_=paired[UPPER:P, 0, :])
        gather(xo_bytes[:], xo_scale_table, note_list, 0, J)
        gather(xo_codes[0][:], xo_table, note_list, 0, HALF)
        deal_bytes(w2_bytes, w2_paired, 0, 1)
        deal_bytes(w_bytes, w_paired, 0, 1)

        hidden = [sbuf(f"hidden{t}", [P, J], F32) for t in range(PACK)]

        def first_product(acc, t, h):
            rows = slice(t * P, (t + 1) * P)
            cols = slice(h * HALF, (h + 1) * HALF)
            nc.tensor.matmul_mx(
                acc, lhsT=w2_dealt[:, rows].bitcast(FP8X4), lhsT_scale=w2_bytes[:, rows],
                rhs=xo_codes[h][:].bitcast(FP4X4), rhs_scale=xo_bytes[:, cols], start=True, stop=False,
            )
            nc.tensor.matmul_mx(
                acc, lhsT=w_dealt[:, rows].bitcast(FP4X4), lhsT_scale=w_bytes[:, rows],
                rhs=xt_codes[h][:].bitcast(FP8X4), rhs_scale=xt_bytes[h][:], start=False, stop=True,
            )

        def put_fine(t, first, count):
            nc.scalar.activation(
                fine[t % FINE_BOARDS][:].indirect(entries(fine_list, first, count)),
                hidden[t][:, first:first + count], COPY,
            )

        acc = psum.tile([P, HALF], F32, name="acc0_first")
        first_product(acc[:], 0, 0)
        nc.scalar.copy(out=hidden[0][:, 0:HALF], in_=acc[:])
        put_fine(0, 0, HALF)
        gather(xo_codes[1][:], xo_table, note_list, HALF, HALF)
        gather(xt_bytes[1][:], xt_scale_table, tok_list, HALF, HALF)
        gather(xt_codes[1][:], xt_table, tok_list, HALF, HALF)
        acc = psum.tile([P, HALF], F32, name="acc0_second")
        first_product(acc[:], 0, 1)
        nc.vector.tensor_copy(out=hidden[0][:, HALF:J], in_=acc[:])
        deal_bytes(w2_bytes, w2_paired, 1, PACK)
        deal_bytes(w_bytes, w_paired, 1, PACK)
        for t in range(1, PACK):
            acc = psum.tile([P, J], F32, name=f"acc{t}")
            for h in range(2):
                first_product(acc[:, h * HALF:(h + 1) * HALF], t, h)
            nc.vector.tensor_copy(out=hidden[t][:], in_=acc[:])

        vs_scale_table = sbuf("vs_scale_table", [P, V], U8, tag="w_dealt")
        nc.gpsimd.memset(vs_scale_table[:].bitcast(I32), 0)
        coarse = [
            sbuf(f"coarse{t}", [P, U], F32, tag=tag)
            for t, tag in enumerate(("xo_codes0", "xt_codes0", "xo_bytes", "xt_bytes0"))
        ]
        for board in coarse:
            nc.gpsimd.memset(board[:], 0.0)

        vs_codes = sbuf("vs_codes", [P, N], U32)
        vs_bytes = sbuf("vs_bytes", [P, N], U8)
        spread(((vs_scale_table, vs_stage),))
        gather(vs_bytes[:], vs_scale_table, store_list, 0, N)
        gather(vs_codes[:], vs_table, store_list, 0, N)

        larger = [sbuf(f"larger{t}", [P, C], F32) for t in range(PACK)]
        picked = [sbuf(f"picked{t}", [P, S], F32) for t in range(PACK)]
        for t in range(PACK):
            nc.scalar.activation(picked[t][:], hidden[t][:].indirect(pick_list[:]), COPY, scale=sa_cols[:, t:t + 1])
            first = HALF if t == 0 else 0
            put_fine(t, first, J - first)
            nc.scalar.activation(coarse[t][:].indirect(coarse_list[:]), picked[t][:], COPY)
            nc.vector.tensor_tensor(
                out=larger[t][:].rearrange("p (u e) -> p u e", e=C // U),
                in0=fine[t % FINE_BOARDS][:].rearrange("p (u e) -> p u e", e=C // U),
                in1=coarse[t][:].unsqueeze(2).to_broadcast([P, U, C // U]),
                op=MAX,
            )

        out_rows = out.rearrange("(b p) o -> p b o", p=P)
        hid = sbuf("hid", [P, PACK, O], BF16)

        def read_board(t, first, count):
            nc.scalar.activation(
                hid[:, t, first:first + count], larger[t][:].indirect(entries(read_list, first, count)), COPY,
                scale=sb_cols[:, t:t + 1],
            )

        woven = sbuf("woven", [P, O, PACK], BF16)

        def weave(tiles, cols):
            nc.vector.tensor_copy(out=woven[:, cols, tiles], in_=hid[:, tiles, cols].rearrange("p t o -> p o t"))

        for t in range(2):
            read_board(t, 0, O)
        weave(slice(0, 2), slice(0, O))
        for h in range(2):
            cols = slice(h * HALF, (h + 1) * HALF)
            for t in range(2, PACK):
                read_board(t, h * HALF, HALF)
            weave(slice(2, PACK), cols)
            hid_codes = sbuf(f"hid_codes{h}", [P, HALF], U32)
            hid_bytes = sbuf(f"hid_bytes{h}", [P, HALF], U8)
            nc.vector.quantize_mx(
                out=hid_codes[:].bitcast(FP8X4), scales=hid_bytes[:],
                in_=woven[:, cols, :].rearrange("p o t -> p (o t)"),
            )

            def second_product(acc, b):
                rows = slice(b * P, (b + 1) * P)
                nc.tensor.matmul_mx(
                    acc, lhsT=vs_codes[:, rows].bitcast(FP8X4), lhsT_scale=vs_bytes[:, rows],
                    rhs=hid_codes[:].bitcast(FP8X4), rhs_scale=hid_bytes[:], start=True, stop=True,
                )

            if h == 0:
                acc = psum.tile([P, 2, HALF], F32, name="y_first")
                for b in range(2):
                    second_product(acc[:, b, :], b)
                result = sbuf("result_first", [P, 2, HALF], F32)
                nc.scalar.copy(out=result[:], in_=acc[:])
                nc.sync.dma_start(out=out_rows[:, :, cols], in_=result[:])
            else:
                for b, copy, queue in ((0, nc.vector.tensor_copy, nc.sync), (1, nc.scalar.copy, nc.scalar)):
                    acc = psum.tile([P, HALF], F32, name=f"y_last{b}")
                    second_product(acc[:], b)
                    result = sbuf(f"result_last{b}", [P, HALF], F32)
                    copy(out=result[:], in_=acc[:])
                    queue.dma_start(out=out_rows[:, b, cols], in_=result[:])
